import numpy as np
import ml_dtypes


def mxq(x, axis, fmt="e4m3"):
    dtype, down = {"e4m3": (ml_dtypes.float8_e4m3fn, 7), "e5m2": (ml_dtypes.float8_e5m2, 14)}[fmt]
    v = np.moveaxis(np.asarray(x, np.float32).astype(ml_dtypes.bfloat16).astype(np.float64), axis, -1)
    blocks = v.reshape(v.shape[:-1] + (-1, 32))
    amax = np.abs(blocks).max(-1, keepdims=True)
    byte = np.maximum(np.where(amax > 0, np.frexp(amax)[1] - 1 + 127, 0) - down, 1)
    scale = np.exp2(byte - 127.0)
    codes = (blocks / scale).astype(np.float32).astype(dtype).astype(np.float64)
    return np.moveaxis((codes * scale).reshape(v.shape), -1, axis)


WIDE = False


def mx_kscale(k):
    if not WIDE:
        return np.ones(k)
    levels = np.array([10, -10, 5, -5, 0])
    if k % 512:
        return np.exp2(np.random.permutation(np.resize(levels, k // 32))).repeat(32)
    a = np.empty((k // 512, 16))
    for p in range(k // 512):
        a[p, :8] = np.random.permutation(np.resize(levels, 8))
        for g in range(8):
            far = levels[np.abs(levels - a[p, g]) >= 10]
            a[p, g + 8] = far[np.random.randint(len(far))]
    return np.exp2(a.ravel()).repeat(32)


def f64(x):
    return np.asarray(x).astype(np.float64)


def striped8(idx):
    return np.asarray(idx).reshape(8, -1, 16).transpose(0, 2, 1).reshape(128, -1).astype(np.uint16)


def unstriped8(offs):
    return offs.reshape(8, 16, -1).transpose(0, 2, 1).reshape(8, -1).astype(np.int64)


def pick8(x, idx, run):
    r = np.arange(len(x))
    return x[r[:, None], idx[r % (8 * run) // run]]


E2M1 = np.array([0.0, 0.5, 1.0, 1.5, 2.0, 3.0, 4.0, 6.0, -0.0, -0.5, -1.0, -1.5, -2.0, -3.0, -4.0, -6.0])


def pack_weight(w, fmt):
    k, n = w.shape
    w = f64(np.asarray(w, np.float32).astype(ml_dtypes.bfloat16)).reshape(k // 32, 32, n)
    amax = np.abs(w).max(1)
    if fmt == "e4m3":
        byte = np.frexp(amax)[1] - 1 + 127 - 7
    else:
        mant, ex = np.frexp(amax / 6.0)
        byte = np.where(mant > 0.5, ex, ex - 1) + 127
    byte = np.clip(np.where(amax > 0, byte, 1), 1, 254)
    scaled = (w * np.exp2(127.0 - byte)[:, None, :]).reshape(k, n).astype(np.float32)
    by_word = np.ascontiguousarray(scaled.reshape(k // 512, 128, 4, n).transpose(0, 1, 3, 2))
    if fmt == "e4m3":
        words = by_word.astype(ml_dtypes.float8_e4m3fn).view(np.uint8)
    else:
        c = by_word.astype(ml_dtypes.float4_e2m1fn).view(np.uint8) & 0xF
        words = (c[..., 0::2] | (c[..., 1::2] << 4)).reshape(k // 512, 128, 2 * n)
    return np.ascontiguousarray(words), np.ascontiguousarray(byte.astype(np.uint8).reshape(k // 512, 16, n))


def unpack_weight(words, scales, fmt):
    g, _, n = scales.shape
    words = np.ascontiguousarray(words).reshape(g, 128, n, -1)
    if fmt == "e4m3":
        vals = words.view(ml_dtypes.float8_e4m3fn).astype(np.float64)
    else:
        nib = np.empty((g, 128, n, 4), np.uint8)
        nib[..., 0::2] = words & 0xF
        nib[..., 1::2] = words >> 4
        vals = E2M1[nib]
    vals = vals * np.repeat(np.exp2(scales.astype(np.float64) - 127.0), 8, axis=1)[..., None]
    return vals.transpose(0, 1, 3, 2).reshape(g * 512, n)


def sigmoid(v):
    return 1.0 / (1.0 + np.exp(-v))


D, T, I, Q, E = 512, 1024, 512, 512, 256


def setup_inputs():
    n = np.random.standard_normal
    idx = np.stack([np.random.permutation(T)[:I] for _ in range(8)])
    idx2 = np.stack([np.random.permutation(T)[:I] for _ in range(8)])
    idx3 = np.stack([np.random.permutation(T)[:I] for _ in range(8)])
    idx4 = np.stack([np.random.permutation(T)[:I] for _ in range(8)])
    fd = mx_kscale(D)
    fq = mx_kscale(Q)
    keysp = pack_weight(n((D, T)) / fd[:, None], "e4m3")
    mixp = pack_weight(n((Q, E)) * 1.0 / np.sqrt(Q) / fq[:, None], "e2m1")
    return {
        "query": (n((D, Q)) * 1.0 / np.sqrt(D) * fd[:, None]).astype(np.float32),
        "keys_words": keysp[0],
        "keys_scales": keysp[1],
        "thr": (np.random.uniform(-0.6, 0.6, (Q, 1))).astype(np.float32),
        "slope": (np.random.uniform(1.0, 3.0, (Q, 1))).astype(np.float32),
        "rowf": (np.random.uniform(0.5, 2.0, (Q, 1)) * fq[:, None]).astype(np.float32),
        "mix_words": mixp[0],
        "mix_scales": mixp[1],
        "offs": striped8(idx),
        "offs2": striped8(idx2),
        "offs3": striped8(idx3),
        "offs4": striped8(idx4),
    }


def reference(query, keys_words, keys_scales, thr, slope, rowf, mix_words, mix_scales, offs, offs2, offs3, offs4):
    idx = unstriped8(offs)
    idx2 = unstriped8(offs2)
    idx3 = unstriped8(offs3)
    idx4 = unstriped8(offs4)
    keysu = unpack_weight(keys_words, keys_scales, "e4m3")
    mixu = unpack_weight(mix_words, mix_scales, "e2m1")
    queryq = mxq(f64(query), 0, "e4m3")
    a = queryq.T @ keysu
    s1 = sigmoid(pick8(a, idx3, 64) * f64(slope) + f64(thr))
    r = pick8(a, idx2, 64) - pick8(a, idx, 64)
    w = r * s1
    f1 = np.zeros((Q, T))
    f1[np.arange(Q)[:, None], idx[np.arange(Q) % 512 // 64]] = w
    f2 = np.zeros((Q, T))
    f2[np.arange(Q)[:, None], idx2[np.arange(Q) % 512 // 64]] = w
    c1 = a + f1
    c2 = c1 - f2
    g = pick8(c2, idx4, 64)
    gw = g * f64(rowf)
    gwq = mxq(gw, 0, "e4m3")
    y = mixu.T @ gwq
    return y

@@ -1,0 +1,247 @@
+from contextlib import ExitStack
+
+import concourse.mybir as mybir
+
+D, T, I, Q, E = 512, 1024, 512, 512, 256
+FLOPS = 2 * D * Q * T + 2 * Q * E * I
+
+F32 = mybir.dt.float32
+BF16 = mybir.dt.bfloat16
+I32 = mybir.dt.int32
+U32 = mybir.dt.uint32
+U16 = mybir.dt.uint16
+U8 = mybir.dt.uint8
+FP8X4 = mybir.dt.float8_e4m3fn_x4
+FP4X4 = mybir.dt.float4_e2m1fn_x4
+ADD = mybir.AluOpType.add
+SUB = mybir.AluOpType.subtract
+MULT = mybir.AluOpType.mult
+COPY = mybir.ActivationFunctionType.Copy
+SIGMOID = mybir.ActivationFunctionType.Sigmoid
+
+P = 128
+PACK = 4
+BANK = 512
+HALF = I // 2
+LIST_COLS = I // 16
+
+
+def tile_attend_gatedswap_one_mixed_kernel(
+    tc, query, keys_words, keys_scales, thr, slope, rowf, mix_words, mix_scales, offs, offs2, offs3, offs4, out
+):
+    nc = tc.nc
+    with ExitStack() as ctx:
+        sb = ctx.enter_context(tc.tile_pool(name="sb", bufs=1))
+        ps = ctx.enter_context(tc.psum_pool(name="ps", bufs=1))
+
+        def new(name, shape, dtype):
+            return sb.tile(shape, dtype, name=name, align_bytes=64)
+
+        def load_list(name, src):
+            lst = sb.tile([P, LIST_COLS], U16, name=name)
+            nc.sync.dma_start(lst[:], src)
+            return lst
+
+        def load_rows(name, src):
+            col = new(name, [P, PACK], F32)
+            nc.sync.dma_start(out=col[:], in_=src.rearrange("(p t) o -> p (t o)", t=PACK))
+            return col
+
+        key_rows = keys_scales[0].bitcast(I32).rearrange("(u v r) c -> u r v c", u=2, v=2)
+        stage = new("key_scale_stage", [P, 2, T // 4], I32)
+        for u in range(2):
+            nc.sync.dma_start(out=stage[64 * u : 64 * u + 4, :, :], in_=key_rows[u])
+        q_raw = new("q_raw", [P, PACK, Q], F32)
+        nc.sync.dma_start(out=q_raw[:], in_=query.rearrange("(p j) q -> p j q", j=PACK))
+        k_codes = new("k_codes", [P, T], U32)
+        nc.sync.dma_start(out=k_codes[:].bitcast(I32), in_=keys_words[0].rearrange("p n t -> p (n t)").bitcast(I32))
+        l1 = load_list("l1", offs)
+        l2 = load_list("l2", offs2)
+        l3 = load_list("l3", offs3)
+        slope_t = load_rows("slope_t", slope)
+        thr_t = load_rows("thr_t", thr)
+        l4 = load_list("l4", offs4)
+        rowf_t = load_rows("rowf_t", rowf)
+        m_codes = new("m_codes", [P, 2 * E], U8)
+        nc.sync.dma_start(out=m_codes[:].bitcast(I32), in_=mix_words[0].bitcast(I32))
+
+        k_scale = new("k_scale", [P, T], U8)
+        nc.vector.memset(k_scale[:].bitcast(I32), 0)
+        m_scale = new("m_scale", [P, E], U8)
+        nc.vector.memset(m_scale[:].bitcast(I32), 0)
+        for quad in range(4):
+            nc.sync.dma_start(
+                out=m_scale[32 * quad : 32 * quad + 4, :].bitcast(I32),
+                in_=mix_scales[0][4 * quad : 4 * quad + 4, :].bitcast(I32),
+            )
+        f1 = [new("f1_%d" % b, [P, T], F32) for b in range(2)]
+        f2 = [new("f2_%d" % b, [P, T], F32) for b in range(2)]
+        for b in range(2):
+            nc.vector.memset(f1[b][:], 0.0)
+            nc.vector.memset(f2[b][:], 0.0)
+        for quad in range(4):
+            u, v = divmod(quad, 2)
+            nc.vector.tensor_copy(
+                out=k_scale[32 * quad : 32 * quad + 4, :].bitcast(I32), in_=stage[64 * u : 64 * u + 4, v, :]
+            )
+
+        q_codes, q_scale = [], []
+        q_dealt = q_raw[:].rearrange("p j (m t) -> p m j t", t=PACK)
+
+        def round_query(pair):
+            qb = new("qb%d" % pair, [P, 2, P, PACK], BF16)
+            nc.vector.tensor_copy(
+                out=qb[:].rearrange("p t m j -> p m j t"), in_=q_dealt[:, :, :, 2 * pair : 2 * pair + 2]
+            )
+            return qb
+
+        def quantise_query(pair, qb):
+            codes = new("q_codes%d" % pair, [P, 2 * P], U32)
+            scale = new("q_scale%d" % pair, [P, 2 * P], U8)
+            nc.vector.quantize_mx(
+                out=codes[:].bitcast(FP8X4), scales=scale[:], in_=qb[:].rearrange("p t m j -> p (t m j)")
+            )
+            q_codes.append(codes)
+            q_scale.append(scale)
+
+        banks = {}
+
+        def scores(t):
+            pair, k = divmod(t, 2)
+            cols = slice(k * P, (k + 1) * P)
+            for n in range(2):
+                bank = ps.tile([P, BANK], F32, name="bank%d" % (2 * t + n))
+                toks = slice(n * BANK, (n + 1) * BANK)
+                nc.tensor.matmul_mx(
+                    out=bank[:],
+                    lhsT=q_codes[pair][:, cols].bitcast(FP8X4),
+                    lhsT_scale=q_scale[pair][:, cols],
+                    rhs=k_codes[:, toks].bitcast(FP8X4),
+                    rhs_scale=k_scale[:, toks],
+                    start=True,
+                    stop=True,
+                )
+                banks[t, n] = bank
+
+        a = [new("a%d" % t, [P, T], F32) for t in range(PACK)]
+        g12 = [new("g12_%d" % t, [P, 2 * I], F32) for t in range(PACK)]
+        rs = [new("rs%d" % t, [P, 2 * I], F32) for t in range(PACK)]
+        w = [new("w%d" % t, [P, I], F32) for t in range(PACK)]
+        c1 = [rs[1], rs[2], rs[3], rs[0]]
+        c2 = [g12[2], g12[3], g12[0], g12[1]]
+        gw = [new("gw%d" % h, [P, PACK, HALF], BF16) for h in range(2)]
+
+        def part(lst, lo, hi):
+            return lst[:, lo // 16 : hi // 16]
+
+        def gate(t, lo, hi):
+            nc.scalar.activation(
+                out=rs[t][:, I + lo : I + hi],
+                in_=a[t][:].indirect(part(l3, lo, hi)),
+                func=SIGMOID,
+                bias=thr_t[:, t : t + 1],
+                scale=slope_t[:, t : t + 1],
+            )
+
+        def fetch_pair(t, lo, hi):
+            nc.scalar.activation(out=g12[t][:, lo:hi], in_=a[t][:].indirect(part(l1, lo, hi)), func=COPY)
+            nc.scalar.activation(out=g12[t][:, I + lo : I + hi], in_=a[t][:].indirect(part(l2, lo, hi)), func=COPY)
+
+        def share(t, lo, hi):
+            nc.gpsimd.tensor_tensor(out=rs[t][:, lo:hi], in0=g12[t][:, I + lo : I + hi], in1=g12[t][:, lo:hi], op=SUB)
+            nc.gpsimd.tensor_tensor(out=w[t][:, lo:hi], in0=rs[t][:, lo:hi], in1=rs[t][:, I + lo : I + hi], op=MULT)
+
+        def place(t, lo, hi):
+            nc.vector.tensor_copy(out=f1[t % 2][:].indirect(part(l1, lo, hi)), in_=w[t][:, lo:hi])
+            nc.vector.tensor_copy(out=f2[t % 2][:].indirect(part(l2, lo, hi)), in_=w[t][:, lo:hi])
+
+        def front(t):
+            for n in range(2):
+                nc.scalar.copy(out=a[t][:, n * BANK : (n + 1) * BANK], in_=banks[t, n][:])
+            fetch_pair(t, 0, I)
+            gate(t, 0, I)
+
+        def add_first(t):
+            nc.gpsimd.tensor_tensor(out=c1[t][:], in0=a[t][:], in1=f1[t % 2][:], op=ADD)
+
+        def take_second(t, engine):
+            engine.tensor_tensor(out=c2[t][:], in0=c1[t][:], in1=f2[t % 2][:], op=SUB)
+
+        def results(t):
+            for h in range(2):
+                nc.scalar.activation(
+                    out=gw[h][:, t, :],
+                    in_=c2[t][:].indirect(part(l4, h * HALF, (h + 1) * HALF)),
+                    func=COPY,
+                    scale=rowf_t[:, t : t + 1],
+                )
+
+        qb0 = round_query(0)
+        quantise_query(0, qb0)
+        scores(0)
+        scores(1)
+        qb1 = round_query(1)
+        for n in range(2):
+            nc.vector.tensor_copy(out=a[0][:, n * BANK : (n + 1) * BANK], in_=banks[0, n][:])
+        gate(0, 0, HALF)
+        nc.vector.tensor_copy(out=g12[0][:, 0:HALF], in_=a[0][:].indirect(part(l1, 0, HALF)))
+        nc.vector.tensor_tensor(out=rs[0][:, 0:HALF], in0=a[0][:].indirect(part(l2, 0, HALF)), in1=g12[0][:, 0:HALF], op=SUB)
+        quantise_query(1, qb1)
+        nc.vector.tensor_tensor(out=w[0][:, 0:HALF], in0=rs[0][:, 0:HALF], in1=rs[0][:, I : I + HALF], op=MULT)
+        scores(2)
+        scores(3)
+        fetch_pair(0, HALF, I)
+        gate(0, HALF, I)
+        share(0, HALF, I)
+        place(0, 0, HALF)
+        front(1)
+        place(0, HALF, I)
+        share(1, 0, I)
+        front(2)
+        front(3)
+        place(1, 0, I)
+        add_first(0)
+        share(2, 0, I)
+        take_second(0, nc.gpsimd)
+        place(2, 0, I)
+        add_first(1)
+        share(3, 0, I)
+        results(0)
+        take_second(1, nc.gpsimd)
+        results(1)
+        place(3, 0, I)
+        add_first(2)
+        take_second(2, nc.gpsimd)
+        results(2)
+        for n in range(2):
+            toks = slice(n * BANK, (n + 1) * BANK)
+            nc.vector.tensor_tensor(out=c1[3][:, toks], in0=banks[3, n][:], in1=f1[1][:, toks], op=ADD)
+        take_second(3, nc.vector)
+        results(3)
+
+        out_v = out.rearrange("(b p) i -> p b i", p=P)
+        for h in range(2):
+            gl = new("gl%d" % h, [P, HALF, PACK], BF16)
+            nc.vector.tensor_copy(
+                out=gl[:].rearrange("p (c i) t -> p c t i", i=4), in_=gw[h][:].rearrange("p t (c i) -> p c t i", i=4)
+            )
+            g_codes = new("g_codes%d" % h, [P, HALF], U32)
+            g_scale = new("g_scale%d" % h, [P, HALF], U8)
+            nc.vector.quantize_mx(out=g_codes[:].bitcast(FP8X4), scales=g_scale[:], in_=gl[:].rearrange("p i t -> p (i t)"))
+            y = new("y%d" % h, [P, 2, HALF], F32)
+            for b in range(2):
+                bank = ps.tile([P, HALF], F32, name="bank%d" % (2 * h + b))
+                nc.tensor.matmul_mx(
+                    out=bank[:],
+                    lhsT=m_codes[:, 2 * P * b : 2 * P * (b + 1)].bitcast(FP4X4),
+                    lhsT_scale=m_scale[:, P * b : P * (b + 1)],
+                    rhs=g_codes[:].bitcast(FP8X4),
+                    rhs_scale=g_scale[:],
+                    start=True,
+                    stop=True,
+                )
+                if h == 1 and b == 1:
+                    nc.vector.tensor_copy(out=y[:, b, :], in_=bank[:])
+                else:
+                    nc.scalar.copy(out=y[:, b, :], in_=bank[:])
+            nc.sync.dma_start(out=out_v[:, :, h * HALF : (h + 1) * HALF], in_=y[:])

@@ -42,26 +42,30 @@ def tile_attend_gatedswap_one_mixed_kernel(
             nc.sync.dma_start(lst[:], src)
             return lst
 
-        def load_rows(name, src):
+        def load_rows(name, src, queue):
             col = new(name, [P, PACK], F32)
-            nc.sync.dma_start(out=col[:], in_=src.rearrange("(p t) o -> p (t o)", t=PACK))
+            queue.dma_start(out=col[:], in_=src.rearrange("(p t) o -> p (t o)", t=PACK))
             return col
 
         key_rows = keys_scales[0].bitcast(I32).rearrange("(u v r) c -> u r v c", u=2, v=2)
         stage = new("key_scale_stage", [P, 2, T // 4], I32)
         for u in range(2):
             nc.sync.dma_start(out=stage[64 * u : 64 * u + 4, :, :], in_=key_rows[u])
-        q_raw = new("q_raw", [P, PACK, Q], F32)
-        nc.sync.dma_start(out=q_raw[:], in_=query.rearrange("(p j) q -> p j q", j=PACK))
-        k_codes = new("k_codes", [P, T], U32)
-        nc.sync.dma_start(out=k_codes[:].bitcast(I32), in_=keys_words[0].rearrange("p n t -> p (n t)").bitcast(I32))
+        q_rows = query.rearrange("(p j) q -> p j q", j=PACK)
+        q_raw = [new("q_raw%d" % s, [P, PACK, Q // 2], F32) for s in range(2)]
+        for s in range(2):
+            nc.sync.dma_start(out=q_raw[s][:], in_=q_rows[:, :, s * Q // 2 : (s + 1) * Q // 2])
+        key_words = keys_words[0].rearrange("p n t -> p (n t)").bitcast(I32)
+        k_codes = [new("k_codes%d" % n, [P, BANK], U32) for n in range(2)]
+        for n in range(2):
+            nc.sync.dma_start(out=k_codes[n][:].bitcast(I32), in_=key_words[:, n * BANK : (n + 1) * BANK])
+        l3 = load_list("l3", offs3)
         l1 = load_list("l1", offs)
         l2 = load_list("l2", offs2)
-        l3 = load_list("l3", offs3)
-        slope_t = load_rows("slope_t", slope)
-        thr_t = load_rows("thr_t", thr)
+        slope_t = load_rows("slope_t", slope, nc.gpsimd)
+        thr_t = load_rows("thr_t", thr, nc.gpsimd)
         l4 = load_list("l4", offs4)
-        rowf_t = load_rows("rowf_t", rowf)
+        rowf_t = load_rows("rowf_t", rowf, nc.sync)
         m_codes = new("m_codes", [P, 2 * E], U8)
         nc.sync.dma_start(out=m_codes[:].bitcast(I32), in_=mix_words[0].bitcast(I32))
 
@@ -76,9 +80,9 @@ def tile_attend_gatedswap_one_mixed_kernel(
             )
         f1 = [new("f1_%d" % b, [P, T], F32) for b in range(2)]
         f2 = [new("f2_%d" % b, [P, T], F32) for b in range(2)]
-        for b in range(2):
-            nc.vector.memset(f1[b][:], 0.0)
-            nc.vector.memset(f2[b][:], 0.0)
+        for b, engine in enumerate((nc.vector, nc.gpsimd)):
+            engine.memset(f1[b][:], 0.0)
+            engine.memset(f2[b][:], 0.0)
         for quad in range(4):
             u, v = divmod(quad, 2)
             nc.vector.tensor_copy(
@@ -86,13 +90,15 @@ def tile_attend_gatedswap_one_mixed_kernel(
             )
 
         q_codes, q_scale = [], []
-        q_dealt = q_raw[:].rearrange("p j (m t) -> p m j t", t=PACK)
 
         def round_query(pair):
             qb = new("qb%d" % pair, [P, 2, P, PACK], BF16)
-            nc.vector.tensor_copy(
-                out=qb[:].rearrange("p t m j -> p m j t"), in_=q_dealt[:, :, :, 2 * pair : 2 * pair + 2]
-            )
+            for s in range(2):
+                dealt = q_raw[s][:].rearrange("p j (m t) -> p m j t", t=PACK)
+                nc.vector.tensor_copy(
+                    out=qb[:, :, s * P // 2 : (s + 1) * P // 2, :].rearrange("p t m j -> p m j t"),
+                    in_=dealt[:, :, :, 2 * pair : 2 * pair + 2],
+                )
             return qb
 
         def quantise_query(pair, qb):
@@ -109,14 +115,15 @@ def tile_attend_gatedswap_one_mixed_kernel(
         def scores(t):
             pair, k = divmod(t, 2)
             cols = slice(k * P, (k + 1) * P)
+            both = ps.tile([P, T], F32, name="score_banks")
             for n in range(2):
-                bank = ps.tile([P, BANK], F32, name="bank%d" % (2 * t + n))
+                bank = both[:, n * BANK : (n + 1) * BANK]
                 toks = slice(n * BANK, (n + 1) * BANK)
                 nc.tensor.matmul_mx(
-                    out=bank[:],
+                    out=bank,
                     lhsT=q_codes[pair][:, cols].bitcast(FP8X4),
                     lhsT_scale=q_scale[pair][:, cols],
-                    rhs=k_codes[:, toks].bitcast(FP8X4),
+                    rhs=k_codes[n][:].bitcast(FP8X4),
                     rhs_scale=k_scale[:, toks],
                     start=True,
                     stop=True,
@@ -124,42 +131,51 @@ def tile_attend_gatedswap_one_mixed_kernel(
                 banks[t, n] = bank
 
         a = [new("a%d" % t, [P, T], F32) for t in range(PACK)]
-        g12 = [new("g12_%d" % t, [P, 2 * I], F32) for t in range(PACK)]
-        rs = [new("rs%d" % t, [P, 2 * I], F32) for t in range(PACK)]
-        w = [new("w%d" % t, [P, I], F32) for t in range(PACK)]
-        c1 = [rs[1], rs[2], rs[3], rs[0]]
-        c2 = [g12[2], g12[3], g12[0], g12[1]]
-        gw = [new("gw%d" % h, [P, PACK, HALF], BF16) for h in range(2)]
+        work = [new("work%d" % k, [P, T], F32) for k in range(2 * PACK)]
+        w = [new("w%d" % k, [P, HALF], F32) for k in range(2 * PACK)]
+        c1 = [work[2], work[5], work[7], work[0]]
+        c2 = [work[3], work[6], work[4], work[1]]
+        gw = [[new("gw%d%d" % (h, pair), [P, 2, HALF], BF16) for pair in range(2)] for h in range(2)]
 
-        def part(lst, lo, hi):
-            return lst[:, lo // 16 : hi // 16]
+        def part(lst, h):
+            return lst[:, h * LIST_COLS // 2 : (h + 1) * LIST_COLS // 2]
 
-        def gate(t, lo, hi):
+        def field(k, f):
+            return work[k][:, f * HALF : (f + 1) * HALF]
+
+        FIRST, SECOND, DIFF, GATE = range(4)
+
+        def gate(k):
+            t, h = divmod(k, 2)
             nc.scalar.activation(
-                out=rs[t][:, I + lo : I + hi],
-                in_=a[t][:].indirect(part(l3, lo, hi)),
+                out=field(k, GATE),
+                in_=a[t][:].indirect(part(l3, h)),
                 func=SIGMOID,
                 bias=thr_t[:, t : t + 1],
                 scale=slope_t[:, t : t + 1],
             )
 
-        def fetch_pair(t, lo, hi):
-            nc.scalar.activation(out=g12[t][:, lo:hi], in_=a[t][:].indirect(part(l1, lo, hi)), func=COPY)
-            nc.scalar.activation(out=g12[t][:, I + lo : I + hi], in_=a[t][:].indirect(part(l2, lo, hi)), func=COPY)
+        def fetch(k):
+            t, h = divmod(k, 2)
+            nc.scalar.activation(out=field(k, FIRST), in_=a[t][:].indirect(part(l1, h)), func=COPY)
+            nc.scalar.activation(out=field(k, SECOND), in_=a[t][:].indirect(part(l2, h)), func=COPY)
+            gate(k)
 
-        def share(t, lo, hi):
-            nc.gpsimd.tensor_tensor(out=rs[t][:, lo:hi], in0=g12[t][:, I + lo : I + hi], in1=g12[t][:, lo:hi], op=SUB)
-            nc.gpsimd.tensor_tensor(out=w[t][:, lo:hi], in0=rs[t][:, lo:hi], in1=rs[t][:, I + lo : I + hi], op=MULT)
+        def share(k):
+            nc.gpsimd.tensor_tensor(out=field(k, DIFF), in0=field(k, SECOND), in1=field(k, FIRST), op=SUB)
+            nc.gpsimd.tensor_tensor(out=w[k][:], in0=field(k, DIFF), in1=field(k, GATE), op=MULT)
 
-        def place(t, lo, hi):
-            nc.vector.tensor_copy(out=f1[t % 2][:].indirect(part(l1, lo, hi)), in_=w[t][:, lo:hi])
-            nc.vector.tensor_copy(out=f2[t % 2][:].indirect(part(l2, lo, hi)), in_=w[t][:, lo:hi])
+        def place(k):
+            t, h = divmod(k, 2)
+            nc.vector.tensor_copy(out=f1[t % 2][:].indirect(part(l1, h)), in_=w[k][:])
+            nc.vector.tensor_copy(out=f2[t % 2][:].indirect(part(l2, h)), in_=w[k][:])
 
         def front(t):
+            scores(t)
             for n in range(2):
-                nc.scalar.copy(out=a[t][:, n * BANK : (n + 1) * BANK], in_=banks[t, n][:])
-            fetch_pair(t, 0, I)
-            gate(t, 0, I)
+                nc.scalar.copy(out=a[t][:, n * BANK : (n + 1) * BANK], in_=banks[t, n])
+            fetch(2 * t)
+            fetch(2 * t + 1)
 
         def add_first(t):
             nc.gpsimd.tensor_tensor(out=c1[t][:], in0=a[t][:], in1=f1[t % 2][:], op=ADD)
@@ -170,8 +186,8 @@ def tile_attend_gatedswap_one_mixed_kernel(
         def results(t):
             for h in range(2):
                 nc.scalar.activation(
-                    out=gw[h][:, t, :],
-                    in_=c2[t][:].indirect(part(l4, h * HALF, (h + 1) * HALF)),
+                    out=gw[h][t // 2][:, t % 2, :],
+                    in_=c2[t][:].indirect(part(l4, h)),
                     func=COPY,
                     scale=rowf_t[:, t : t + 1],
                 )
@@ -179,56 +195,62 @@ def tile_attend_gatedswap_one_mixed_kernel(
         qb0 = round_query(0)
         quantise_query(0, qb0)
         scores(0)
-        scores(1)
         qb1 = round_query(1)
         for n in range(2):
-            nc.vector.tensor_copy(out=a[0][:, n * BANK : (n + 1) * BANK], in_=banks[0, n][:])
-        gate(0, 0, HALF)
-        nc.vector.tensor_copy(out=g12[0][:, 0:HALF], in_=a[0][:].indirect(part(l1, 0, HALF)))
-        nc.vector.tensor_tensor(out=rs[0][:, 0:HALF], in0=a[0][:].indirect(part(l2, 0, HALF)), in1=g12[0][:, 0:HALF], op=SUB)
+            nc.vector.tensor_copy(out=a[0][:, n * BANK : (n + 1) * BANK], in_=banks[0, n])
+        gate(0)
+        nc.vector.tensor_copy(out=field(0, FIRST), in_=a[0][:].indirect(part(l1, 0)))
+        nc.vector.tensor_tensor(out=field(0, DIFF), in0=a[0][:].indirect(part(l2, 0)), in1=field(0, FIRST), op=SUB)
         quantise_query(1, qb1)
-        nc.vector.tensor_tensor(out=w[0][:, 0:HALF], in0=rs[0][:, 0:HALF], in1=rs[0][:, I : I + HALF], op=MULT)
-        scores(2)
-        scores(3)
-        fetch_pair(0, HALF, I)
-        gate(0, HALF, I)
-        share(0, HALF, I)
-        place(0, 0, HALF)
+        nc.vector.tensor_tensor(out=w[0][:], in0=field(0, DIFF), in1=field(0, GATE), op=MULT)
+        fetch(1)
+        share(1)
+        place(0)
         front(1)
-        place(0, HALF, I)
-        share(1, 0, I)
         front(2)
         front(3)
-        place(1, 0, I)
+        place(1)
+        share(2)
         add_first(0)
-        share(2, 0, I)
+        place(2)
+        share(3)
         take_second(0, nc.gpsimd)
-        place(2, 0, I)
+        place(3)
+        share(4)
+        share(5)
         add_first(1)
-        share(3, 0, I)
-        results(0)
+        place(4)
+        share(6)
         take_second(1, nc.gpsimd)
+        place(5)
+        share(7)
+        results(0)
         results(1)
-        place(3, 0, I)
+        place(6)
         add_first(2)
         take_second(2, nc.gpsimd)
         results(2)
+        place(7)
         for n in range(2):
             toks = slice(n * BANK, (n + 1) * BANK)
-            nc.vector.tensor_tensor(out=c1[3][:, toks], in0=banks[3, n][:], in1=f1[1][:, toks], op=ADD)
+            nc.vector.tensor_tensor(out=c1[3][:, toks], in0=banks[3, n], in1=f1[1][:, toks], op=ADD)
         take_second(3, nc.vector)
         results(3)
 
-        out_v = out.rearrange("(b p) i -> p b i", p=P)
+        woven = [c1[3][:, h * BANK : (h + 1) * BANK].bitcast(BF16) for h in range(2)]
+        for pair in range(2):
+            for h in range(2):
+                ts = slice(2 * pair, 2 * pair + 2)
+                nc.vector.tensor_copy(
+                    out=woven[h].rearrange("p (c i t) -> p c t i", i=4, t=PACK)[:, :, ts, :],
+                    in_=gw[h][pair][:].rearrange("p t (c i) -> p c t i", i=4),
+                )
         for h in range(2):
-            gl = new("gl%d" % h, [P, HALF, PACK], BF16)
-            nc.vector.tensor_copy(
-                out=gl[:].rearrange("p (c i) t -> p c t i", i=4), in_=gw[h][:].rearrange("p t (c i) -> p c t i", i=4)
-            )
             g_codes = new("g_codes%d" % h, [P, HALF], U32)
             g_scale = new("g_scale%d" % h, [P, HALF], U8)
-            nc.vector.quantize_mx(out=g_codes[:].bitcast(FP8X4), scales=g_scale[:], in_=gl[:].rearrange("p i t -> p (i t)"))
-            y = new("y%d" % h, [P, 2, HALF], F32)
+            nc.vector.quantize_mx(
+                out=g_codes[:].bitcast(FP8X4), scales=g_scale[:], in_=woven[h]
+            )
             for b in range(2):
                 bank = ps.tile([P, HALF], F32, name="bank%d" % (2 * h + b))
                 nc.tensor.matmul_mx(
@@ -240,8 +262,9 @@ def tile_attend_gatedswap_one_mixed_kernel(
                     start=True,
                     stop=True,
                 )
+                y = new("y%d%d" % (h, b), [P, HALF], F32)
                 if h == 1 and b == 1:
-                    nc.vector.tensor_copy(out=y[:, b, :], in_=bank[:])
+                    nc.vector.tensor_copy(out=y[:], in_=bank[:])
                 else:
-                    nc.scalar.copy(out=y[:, b, :], in_=bank[:])
-            nc.sync.dma_start(out=out_v[:, :, h * HALF : (h + 1) * HALF], in_=y[:])
+                    nc.scalar.copy(out=y[:], in_=bank[:])
+                nc.sync.dma_start(out=out[b * P : (b + 1) * P, h * HALF : (h + 1) * HALF], in_=y[:])

@@ -24,6 +24,9 @@ PACK = 4
 BANK = 512
 HALF = I // 2
 LIST_COLS = I // 16
+QUAD = 32
+SCALE_ROWS = 4
+FIRST, SECOND, DIFF, GATE = range(4)
 
 
 def tile_attend_gatedswap_one_mixed_kernel(
@@ -50,20 +53,18 @@ def tile_attend_gatedswap_one_mixed_kernel(
         key_rows = keys_scales[0].bitcast(I32).rearrange("(u v r) c -> u r v c", u=2, v=2)
         stage = new("key_scale_stage", [P, 2, T // 4], I32)
         for u in range(2):
-            nc.sync.dma_start(out=stage[64 * u : 64 * u + 4, :, :], in_=key_rows[u])
-        q_rows = query.rearrange("(p j) q -> p j q", j=PACK)
-        q_raw = [new("q_raw%d" % s, [P, PACK, Q // 2], F32) for s in range(2)]
-        for s in range(2):
-            nc.sync.dma_start(out=q_raw[s][:], in_=q_rows[:, :, s * Q // 2 : (s + 1) * Q // 2])
+            nc.scalar.dma_start(out=stage[2 * QUAD * u : 2 * QUAD * u + SCALE_ROWS, :, :], in_=key_rows[u])
+        slope_t = load_rows("slope_t", slope, nc.scalar)
+        thr_t = load_rows("thr_t", thr, nc.scalar)
+        l3 = load_list("l3", offs3)
+        q_raw = new("q_raw", [P, PACK, Q], F32)
+        nc.sync.dma_start(out=q_raw[:], in_=query.rearrange("(p j) q -> p j q", j=PACK))
         key_words = keys_words[0].rearrange("p n t -> p (n t)").bitcast(I32)
         k_codes = [new("k_codes%d" % n, [P, BANK], U32) for n in range(2)]
         for n in range(2):
             nc.sync.dma_start(out=k_codes[n][:].bitcast(I32), in_=key_words[:, n * BANK : (n + 1) * BANK])
-        l3 = load_list("l3", offs3)
         l1 = load_list("l1", offs)
         l2 = load_list("l2", offs2)
-        slope_t = load_rows("slope_t", slope, nc.gpsimd)
-        thr_t = load_rows("thr_t", thr, nc.gpsimd)
         l4 = load_list("l4", offs4)
         rowf_t = load_rows("rowf_t", rowf, nc.sync)
         m_codes = new("m_codes", [P, 2 * E], U8)
@@ -73,32 +74,31 @@ def tile_attend_gatedswap_one_mixed_kernel(
         nc.vector.memset(k_scale[:].bitcast(I32), 0)
         m_scale = new("m_scale", [P, E], U8)
         nc.vector.memset(m_scale[:].bitcast(I32), 0)
-        for quad in range(4):
+        for quad in range(P // QUAD):
             nc.sync.dma_start(
-                out=m_scale[32 * quad : 32 * quad + 4, :].bitcast(I32),
-                in_=mix_scales[0][4 * quad : 4 * quad + 4, :].bitcast(I32),
+                out=m_scale[QUAD * quad : QUAD * quad + SCALE_ROWS, :].bitcast(I32),
+                in_=mix_scales[0][SCALE_ROWS * quad : SCALE_ROWS * (quad + 1), :].bitcast(I32),
             )
         f1 = [new("f1_%d" % b, [P, T], F32) for b in range(2)]
         f2 = [new("f2_%d" % b, [P, T], F32) for b in range(2)]
         for b, engine in enumerate((nc.vector, nc.gpsimd)):
             engine.memset(f1[b][:], 0.0)
             engine.memset(f2[b][:], 0.0)
-        for quad in range(4):
+        for quad in range(P // QUAD):
             u, v = divmod(quad, 2)
             nc.vector.tensor_copy(
-                out=k_scale[32 * quad : 32 * quad + 4, :].bitcast(I32), in_=stage[64 * u : 64 * u + 4, v, :]
+                out=k_scale[QUAD * quad : QUAD * quad + SCALE_ROWS, :].bitcast(I32),
+                in_=stage[2 * QUAD * u : 2 * QUAD * u + SCALE_ROWS, v, :],
             )
 
         q_codes, q_scale = [], []
 
         def round_query(pair):
             qb = new("qb%d" % pair, [P, 2, P, PACK], BF16)
-            for s in range(2):
-                dealt = q_raw[s][:].rearrange("p j (m t) -> p m j t", t=PACK)
-                nc.vector.tensor_copy(
-                    out=qb[:, :, s * P // 2 : (s + 1) * P // 2, :].rearrange("p t m j -> p m j t"),
-                    in_=dealt[:, :, :, 2 * pair : 2 * pair + 2],
-                )
+            dealt = q_raw[:].rearrange("p j (m t) -> p m j t", t=PACK)
+            nc.vector.tensor_copy(
+                out=qb[:].rearrange("p t m j -> p m j t"), in_=dealt[:, :, :, 2 * pair : 2 * pair + 2]
+            )
             return qb
 
         def quantise_query(pair, qb):
@@ -113,8 +113,8 @@ def tile_attend_gatedswap_one_mixed_kernel(
         banks = {}
 
         def scores(t):
-            pair, k = divmod(t, 2)
-            cols = slice(k * P, (k + 1) * P)
+            pair, member = divmod(t, 2)
+            cols = slice(member * P, (member + 1) * P)
             both = ps.tile([P, T], F32, name="score_banks")
             for n in range(2):
                 bank = both[:, n * BANK : (n + 1) * BANK]
@@ -135,15 +135,13 @@ def tile_attend_gatedswap_one_mixed_kernel(
         w = [new("w%d" % k, [P, HALF], F32) for k in range(2 * PACK)]
         c1 = [work[2], work[5], work[7], work[0]]
         c2 = [work[3], work[6], work[4], work[1]]
-        gw = [[new("gw%d%d" % (h, pair), [P, 2, HALF], BF16) for pair in range(2)] for h in range(2)]
+        gw = [new("gw%d" % h, [P, PACK, HALF], BF16) for h in range(2)]
 
         def part(lst, h):
             return lst[:, h * LIST_COLS // 2 : (h + 1) * LIST_COLS // 2]
 
         def field(k, f):
             return work[k][:, f * HALF : (f + 1) * HALF]
-
-        FIRST, SECOND, DIFF, GATE = range(4)
 
         def gate(k):
             t, h = divmod(k, 2)
@@ -186,7 +184,7 @@ def tile_attend_gatedswap_one_mixed_kernel(
         def results(t):
             for h in range(2):
                 nc.scalar.activation(
-                    out=gw[h][t // 2][:, t % 2, :],
+                    out=gw[h][:, t, :],
                     in_=c2[t][:].indirect(part(l4, h)),
                     func=COPY,
                     scale=rowf_t[:, t : t + 1],
@@ -206,9 +204,8 @@ def tile_attend_gatedswap_one_mixed_kernel(
         fetch(1)
         share(1)
         place(0)
-        front(1)
-        front(2)
-        front(3)
+        for t in range(1, PACK):
+            front(t)
         place(1)
         share(2)
         add_first(0)
@@ -231,40 +228,36 @@ def tile_attend_gatedswap_one_mixed_kernel(
         take_second(2, nc.gpsimd)
         results(2)
         place(7)
+        last = PACK - 1
         for n in range(2):
             toks = slice(n * BANK, (n + 1) * BANK)
-            nc.vector.tensor_tensor(out=c1[3][:, toks], in0=banks[3, n], in1=f1[1][:, toks], op=ADD)
-        take_second(3, nc.vector)
-        results(3)
+            nc.vector.tensor_tensor(out=c1[last][:, toks], in0=banks[last, n], in1=f1[last % 2][:, toks], op=ADD)
+        take_second(last, nc.vector)
+        results(last)
 
-        woven = [c1[3][:, h * BANK : (h + 1) * BANK].bitcast(BF16) for h in range(2)]
-        for pair in range(2):
-            for h in range(2):
-                ts = slice(2 * pair, 2 * pair + 2)
-                nc.vector.tensor_copy(
-                    out=woven[h].rearrange("p (c i t) -> p c t i", i=4, t=PACK)[:, :, ts, :],
-                    in_=gw[h][pair][:].rearrange("p t (c i) -> p c t i", i=4),
-                )
         for h in range(2):
+            woven = new("woven%d" % h, [P, HALF * PACK], BF16)
+            nc.vector.tensor_copy(
+                out=woven[:].rearrange("p (c i t) -> p c t i", i=4, t=PACK),
+                in_=gw[h][:].rearrange("p t (c i) -> p c t i", i=4),
+            )
             g_codes = new("g_codes%d" % h, [P, HALF], U32)
             g_scale = new("g_scale%d" % h, [P, HALF], U8)
-            nc.vector.quantize_mx(
-                out=g_codes[:].bitcast(FP8X4), scales=g_scale[:], in_=woven[h]
-            )
-            for b in range(2):
-                bank = ps.tile([P, HALF], F32, name="bank%d" % (2 * h + b))
+            nc.vector.quantize_mx(out=g_codes[:].bitcast(FP8X4), scales=g_scale[:], in_=woven[:])
+            for eb in range(E // P):
+                bank = ps.tile([P, HALF], F32, name="bank%d" % (2 * h + eb))
                 nc.tensor.matmul_mx(
                     out=bank[:],
-                    lhsT=m_codes[:, 2 * P * b : 2 * P * (b + 1)].bitcast(FP4X4),
-                    lhsT_scale=m_scale[:, P * b : P * (b + 1)],
+                    lhsT=m_codes[:, 2 * P * eb : 2 * P * (eb + 1)].bitcast(FP4X4),
+                    lhsT_scale=m_scale[:, P * eb : P * (eb + 1)],
                     rhs=g_codes[:].bitcast(FP8X4),
                     rhs_scale=g_scale[:],
                     start=True,
                     stop=True,
                 )
-                y = new("y%d%d" % (h, b), [P, HALF], F32)
-                if h == 1 and b == 1:
+                y = new("y%d%d" % (h, eb), [P, HALF], F32)
+                if (h, eb) == (1, 1):
                     nc.vector.tensor_copy(out=y[:], in_=bank[:])
                 else:
                     nc.scalar.copy(out=y[:], in_=bank[:])
-                nc.sync.dma_start(out=out[b * P : (b + 1) * P, h * HALF : (h + 1) * HALF], in_=y[:])
+                nc.sync.dma_start(out=out[eb * P : (eb + 1) * P, h * HALF : (h + 1) * HALF], in_=y[:])

from contextlib import ExitStack

import concourse.mybir as mybir

D, T, I, Q, E = 512, 1024, 512, 512, 256
FLOPS = 2 * D * Q * T + 2 * Q * E * I

F32 = mybir.dt.float32
BF16 = mybir.dt.bfloat16
I32 = mybir.dt.int32
U32 = mybir.dt.uint32
U16 = mybir.dt.uint16
U8 = mybir.dt.uint8
FP8X4 = mybir.dt.float8_e4m3fn_x4
FP4X4 = mybir.dt.float4_e2m1fn_x4
ADD = mybir.AluOpType.add
SUB = mybir.AluOpType.subtract
MULT = mybir.AluOpType.mult
COPY = mybir.ActivationFunctionType.Copy
SIGMOID = mybir.ActivationFunctionType.Sigmoid

P = 128
PACK = 4
BANK = 512
HALF = I // 2
LIST_COLS = I // 16
QUAD = 32
SCALE_ROWS = 4
FIRST, SECOND, DIFF, GATE = range(4)


def tile_attend_gatedswap_one_mixed_kernel(
    tc, query, keys_words, keys_scales, thr, slope, rowf, mix_words, mix_scales, offs, offs2, offs3, offs4, out
):
    nc = tc.nc
    with ExitStack() as ctx:
        sb = ctx.enter_context(tc.tile_pool(name="sb", bufs=1))
        ps = ctx.enter_context(tc.psum_pool(name="ps", bufs=1))

        def new(name, shape, dtype):
            return sb.tile(shape, dtype, name=name, align_bytes=64)

        def load_list(name, src):
            lst = sb.tile([P, LIST_COLS], U16, name=name)
            nc.sync.dma_start(lst[:], src)
            return lst

        def load_rows(name, src, queue):
            col = new(name, [P, PACK], F32)
            queue.dma_start(out=col[:], in_=src.rearrange("(p t) o -> p (t o)", t=PACK))
            return col

        key_rows = keys_scales[0].bitcast(I32).rearrange("(u v r) c -> u r v c", u=2, v=2)
        stage = new("key_scale_stage", [P, 2, T // 4], I32)
        for u in range(2):
            nc.scalar.dma_start(out=stage[2 * QUAD * u : 2 * QUAD * u + SCALE_ROWS, :, :], in_=key_rows[u])
        slope_t = load_rows("slope_t", slope, nc.scalar)
        thr_t = load_rows("thr_t", thr, nc.scalar)
        l3 = load_list("l3", offs3)
        q_raw = new("q_raw", [P, PACK, Q], F32)
        nc.sync.dma_start(out=q_raw[:], in_=query.rearrange("(p j) q -> p j q", j=PACK))
        key_words = keys_words[0].rearrange("p n t -> p (n t)").bitcast(I32)
        k_codes = [new("k_codes%d" % n, [P, BANK], U32) for n in range(2)]
        for n in range(2):
            nc.sync.dma_start(out=k_codes[n][:].bitcast(I32), in_=key_words[:, n * BANK : (n + 1) * BANK])
        l1 = load_list("l1", offs)
        l2 = load_list("l2", offs2)
        l4 = load_list("l4", offs4)
        rowf_t = load_rows("rowf_t", rowf, nc.sync)
        m_codes = new("m_codes", [P, 2 * E], U8)
        nc.sync.dma_start(out=m_codes[:].bitcast(I32), in_=mix_words[0].bitcast(I32))

        k_scale = new("k_scale", [P, T], U8)
        nc.vector.memset(k_scale[:].bitcast(I32), 0)
        m_scale = new("m_scale", [P, E], U8)
        nc.vector.memset(m_scale[:].bitcast(I32), 0)
        for quad in range(P // QUAD):
            nc.sync.dma_start(
                out=m_scale[QUAD * quad : QUAD * quad + SCALE_ROWS, :].bitcast(I32),
                in_=mix_scales[0][SCALE_ROWS * quad : SCALE_ROWS * (quad + 1), :].bitcast(I32),
            )
        f1 = [new("f1_%d" % b, [P, T], F32) for b in range(2)]
        f2 = [new("f2_%d" % b, [P, T], F32) for b in range(2)]
        for b, engine in enumerate((nc.vector, nc.gpsimd)):
            engine.memset(f1[b][:], 0.0)
            engine.memset(f2[b][:], 0.0)
        for quad in range(P // QUAD):
            u, v = divmod(quad, 2)
            nc.vector.tensor_copy(
                out=k_scale[QUAD * quad : QUAD * quad + SCALE_ROWS, :].bitcast(I32),
                in_=stage[2 * QUAD * u : 2 * QUAD * u + SCALE_ROWS, v, :],
            )

        q_codes, q_scale = [], []

        def round_query(pair):
            qb = new("qb%d" % pair, [P, 2, P, PACK], BF16)
            dealt = q_raw[:].rearrange("p j (m t) -> p m j t", t=PACK)
            nc.vector.tensor_copy(
                out=qb[:].rearrange("p t m j -> p m j t"), in_=dealt[:, :, :, 2 * pair : 2 * pair + 2]
            )
            return qb

        def quantise_query(pair, qb):
            codes = new("q_codes%d" % pair, [P, 2 * P], U32)
            scale = new("q_scale%d" % pair, [P, 2 * P], U8)
            nc.vector.quantize_mx(
                out=codes[:].bitcast(FP8X4), scales=scale[:], in_=qb[:].rearrange("p t m j -> p (t m j)")
            )
            q_codes.append(codes)
            q_scale.append(scale)

        banks = {}

        def scores(t):
            pair, member = divmod(t, 2)
            cols = slice(member * P, (member + 1) * P)
            both = ps.tile([P, T], F32, name="score_banks")
            for n in range(2):
                bank = both[:, n * BANK : (n + 1) * BANK]
                toks = slice(n * BANK, (n + 1) * BANK)
                nc.tensor.matmul_mx(
                    out=bank,
                    lhsT=q_codes[pair][:, cols].bitcast(FP8X4),
                    lhsT_scale=q_scale[pair][:, cols],
                    rhs=k_codes[n][:].bitcast(FP8X4),
                    rhs_scale=k_scale[:, toks],
                    start=True,
                    stop=True,
                )
                banks[t, n] = bank

        a = [new("a%d" % t, [P, T], F32) for t in range(PACK)]
        work = [new("work%d" % k, [P, T], F32) for k in range(2 * PACK)]
        w = [new("w%d" % k, [P, HALF], F32) for k in range(2 * PACK)]
        c1 = [work[2], work[5], work[7], work[0]]
        c2 = [work[3], work[6], work[4], work[1]]
        gw = [new("gw%d" % h, [P, PACK, HALF], BF16) for h in range(2)]

        def part(lst, h):
            return lst[:, h * LIST_COLS // 2 : (h + 1) * LIST_COLS // 2]

        def field(k, f):
            return work[k][:, f * HALF : (f + 1) * HALF]

        def gate(k):
            t, h = divmod(k, 2)
            nc.scalar.activation(
                out=field(k, GATE),
                in_=a[t][:].indirect(part(l3, h)),
                func=SIGMOID,
                bias=thr_t[:, t : t + 1],
                scale=slope_t[:, t : t + 1],
            )

        def fetch(k):
            t, h = divmod(k, 2)
            nc.scalar.activation(out=field(k, FIRST), in_=a[t][:].indirect(part(l1, h)), func=COPY)
            nc.scalar.activation(out=field(k, SECOND), in_=a[t][:].indirect(part(l2, h)), func=COPY)
            gate(k)

        def share(k):
            nc.gpsimd.tensor_tensor(out=field(k, DIFF), in0=field(k, SECOND), in1=field(k, FIRST), op=SUB)
            nc.gpsimd.tensor_tensor(out=w[k][:], in0=field(k, DIFF), in1=field(k, GATE), op=MULT)

        def place(k):
            t, h = divmod(k, 2)
            nc.vector.tensor_copy(out=f1[t % 2][:].indirect(part(l1, h)), in_=w[k][:])
            nc.vector.tensor_copy(out=f2[t % 2][:].indirect(part(l2, h)), in_=w[k][:])

        def front(t):
            scores(t)
            for n in range(2):
                nc.scalar.copy(out=a[t][:, n * BANK : (n + 1) * BANK], in_=banks[t, n])
            fetch(2 * t)
            fetch(2 * t + 1)

        def add_first(t):
            nc.gpsimd.tensor_tensor(out=c1[t][:], in0=a[t][:], in1=f1[t % 2][:], op=ADD)

        def take_second(t, engine):
            engine.tensor_tensor(out=c2[t][:], in0=c1[t][:], in1=f2[t % 2][:], op=SUB)

        def results(t):
            for h in range(2):
                nc.scalar.activation(
                    out=gw[h][:, t, :],
                    in_=c2[t][:].indirect(part(l4, h)),
                    func=COPY,
                    scale=rowf_t[:, t : t + 1],
                )

        qb0 = round_query(0)
        quantise_query(0, qb0)
        scores(0)
        qb1 = round_query(1)
        for n in range(2):
            nc.vector.tensor_copy(out=a[0][:, n * BANK : (n + 1) * BANK], in_=banks[0, n])
        gate(0)
        nc.vector.tensor_copy(out=field(0, FIRST), in_=a[0][:].indirect(part(l1, 0)))
        nc.vector.tensor_tensor(out=field(0, DIFF), in0=a[0][:].indirect(part(l2, 0)), in1=field(0, FIRST), op=SUB)
        quantise_query(1, qb1)
        nc.vector.tensor_tensor(out=w[0][:], in0=field(0, DIFF), in1=field(0, GATE), op=MULT)
        fetch(1)
        share(1)
        place(0)
        for t in range(1, PACK):
            front(t)
        place(1)
        share(2)
        add_first(0)
        place(2)
        share(3)
        take_second(0, nc.gpsimd)
        place(3)
        share(4)
        share(5)
        add_first(1)
        place(4)
        share(6)
        take_second(1, nc.gpsimd)
        place(5)
        share(7)
        results(0)
        results(1)
        place(6)
        add_first(2)
        take_second(2, nc.gpsimd)
        results(2)
        place(7)
        last = PACK - 1
        for n in range(2):
            toks = slice(n * BANK, (n + 1) * BANK)
            nc.vector.tensor_tensor(out=c1[last][:, toks], in0=banks[last, n], in1=f1[last % 2][:, toks], op=ADD)
        take_second(last, nc.vector)
        results(last)

        for h in range(2):
            woven = new("woven%d" % h, [P, HALF * PACK], BF16)
            nc.vector.tensor_copy(
                out=woven[:].rearrange("p (c i t) -> p c t i", i=4, t=PACK),
                in_=gw[h][:].rearrange("p t (c i) -> p c t i", i=4),
            )
            g_codes = new("g_codes%d" % h, [P, HALF], U32)
            g_scale = new("g_scale%d" % h, [P, HALF], U8)
            nc.vector.quantize_mx(out=g_codes[:].bitcast(FP8X4), scales=g_scale[:], in_=woven[:])
            for eb in range(E // P):
                bank = ps.tile([P, HALF], F32, name="bank%d" % (2 * h + eb))
                nc.tensor.matmul_mx(
                    out=bank[:],
                    lhsT=m_codes[:, 2 * P * eb : 2 * P * (eb + 1)].bitcast(FP4X4),
                    lhsT_scale=m_scale[:, P * eb : P * (eb + 1)],
                    rhs=g_codes[:].bitcast(FP8X4),
                    rhs_scale=g_scale[:],
                    start=True,
                    stop=True,
                )
                y = new("y%d%d" % (h, eb), [P, HALF], F32)
                if (h, eb) == (1, 1):
                    nc.vector.tensor_copy(out=y[:], in_=bank[:])
                else:
                    nc.scalar.copy(out=y[:], in_=bank[:])
                nc.sync.dma_start(out=out[eb * P : (eb + 1) * P, h * HALF : (h + 1) * HALF], in_=y[:])
